import numpy as np
import ml_dtypes


def mxq(x, axis, fmt="e4m3"):
    dtype, down = {"e4m3": (ml_dtypes.float8_e4m3fn, 7), "e5m2": (ml_dtypes.float8_e5m2, 14)}[fmt]
    v = np.moveaxis(np.asarray(x, np.float32).astype(ml_dtypes.bfloat16).astype(np.float64), axis, -1)
    blocks = v.reshape(v.shape[:-1] + (-1, 32))
    amax = np.abs(blocks).max(-1, keepdims=True)
    byte = np.maximum(np.where(amax > 0, np.frexp(amax)[1] - 1 + 127, 0) - down, 1)
    scale = np.exp2(byte - 127.0)
    codes = (blocks / scale).astype(np.float32).astype(dtype).astype(np.float64)
    return np.moveaxis((codes * scale).reshape(v.shape), -1, axis)


WIDE = False


def mx_kscale(k):
    if not WIDE:
        return np.ones(k)
    levels = np.array([10, -10, 5, -5, 0])
    if k % 512:
        return np.exp2(np.random.permutation(np.resize(levels, k // 32))).repeat(32)
    a = np.empty((k // 512, 16))
    for p in range(k // 512):
        a[p, :8] = np.random.permutation(np.resize(levels, 8))
        for g in range(8):
            far = levels[np.abs(levels - a[p, g]) >= 10]
            a[p, g + 8] = far[np.random.randint(len(far))]
    return np.exp2(a.ravel()).repeat(32)


def f64(x):
    return np.asarray(x).astype(np.float64)


def striped(idx):
    return np.tile(idx.reshape(-1, 16).T, (8, 1)).astype(np.uint16)


def unstriped(offs):
    return offs[:16].T.reshape(-1).astype(np.int64)


E2M1 = np.array([0.0, 0.5, 1.0, 1.5, 2.0, 3.0, 4.0, 6.0, -0.0, -0.5, -1.0, -1.5, -2.0, -3.0, -4.0, -6.0])


def pack_weight(w, fmt):
    k, n = w.shape
    w = f64(np.asarray(w, np.float32).astype(ml_dtypes.bfloat16)).reshape(k // 32, 32, n)
    amax = np.abs(w).max(1)
    if fmt == "e4m3":
        byte = np.frexp(amax)[1] - 1 + 127 - 7
    else:
        mant, ex = np.frexp(amax / 6.0)
        byte = np.where(mant > 0.5, ex, ex - 1) + 127
    byte = np.clip(np.where(amax > 0, byte, 1), 1, 254)
    scaled = (w * np.exp2(127.0 - byte)[:, None, :]).reshape(k, n).astype(np.float32)
    by_word = np.ascontiguousarray(scaled.reshape(k // 512, 128, 4, n).transpose(0, 1, 3, 2))
    if fmt == "e4m3":
        words = by_word.astype(ml_dtypes.float8_e4m3fn).view(np.uint8)
    else:
        c = by_word.astype(ml_dtypes.float4_e2m1fn).view(np.uint8) & 0xF
        words = (c[..., 0::2] | (c[..., 1::2] << 4)).reshape(k // 512, 128, 2 * n)
    return np.ascontiguousarray(words), np.ascontiguousarray(byte.astype(np.uint8).reshape(k // 512, 16, n))


def unpack_weight(words, scales, fmt):
    g, _, n = scales.shape
    words = np.ascontiguousarray(words).reshape(g, 128, n, -1)
    if fmt == "e4m3":
        vals = words.view(ml_dtypes.float8_e4m3fn).astype(np.float64)
    else:
        nib = np.empty((g, 128, n, 4), np.uint8)
        nib[..., 0::2] = words & 0xF
        nib[..., 1::2] = words >> 4
        vals = E2M1[nib]
    vals = vals * np.repeat(np.exp2(scales.astype(np.float64) - 127.0), 8, axis=1)[..., None]
    return vals.transpose(0, 1, 3, 2).reshape(g * 512, n)


def gelu(v):
    return 0.5 * v * (1.0 + np.tanh(np.sqrt(2.0 / np.pi) * (v + 0.044715 * v**3)))


K, T, S, H, N, P1, P2, P3 = 1024, 4096, 2048, 512, 768, 1024, 512, 256

def setup_inputs():
    n = np.random.standard_normal
    s = mx_kscale(K)[:, None]
    u = mx_kscale(H)[:, None]
    tab_words, tab_scales = pack_weight((0.5 * n((K, T)) + 0.6 * n((K, 1))) * s, "e4m3")
    w4_words, w4_scales = pack_weight(n((H, N)) / np.sqrt(H) / u, "e2m1")
    return {
        "tab_words": tab_words, "tab_scales": tab_scales,
        "offs": striped(np.random.permutation(T)[:S]),
        "pos1": striped(np.random.permutation(S)[:P1]),
        "pos2": striped(np.random.permutation(S)[:P1]),
        "pos3": striped(np.random.permutation(P1)[:P2]),
        "pos4": striped(np.random.permutation(P1)[:P2]),
        "pos5": striped(np.random.permutation(P2)[:P3]),
        "pos6": striped(np.random.permutation(P2)[:P3]),
        "w1": (n((K, H)) / np.sqrt(K) / s).astype(np.float32),
        "freq": np.random.uniform(0.5, 0.8, H).astype(np.float32),
        "gain": (np.random.uniform(1.0, 3.0, H) * u[:, 0]).astype(np.float32),
        "w4_words": w4_words, "w4_scales": w4_scales,
    }

def reference(tab_words, tab_scales, offs, pos1, pos2, pos3, pos4, pos5, pos6,
              w1, freq, gain, w4_words, w4_scales):
    v = unpack_weight(tab_words, tab_scales, "e4m3")[:, unstriped(offs)]
    w4 = unpack_weight(w4_words, w4_scales, "e2m1")
    h = np.sin(f64(freq)[:, None] * (mxq(f64(w1), 0, "e4m3").T @ v))
    duel = h[:, unstriped(pos1)] * h[:, unstriped(pos2)]
    bench = np.maximum(duel[:, unstriped(pos3)], duel[:, unstriped(pos4)])
    bracket = bench[:, unstriped(pos5)] + bench[:, unstriped(pos6)]
    z = np.tanh(bracket) * f64(gain)[:, None]
    return w4.T @ mxq(z, 0, "e4m3")

@@ -1,0 +1,258 @@
+import math
+from contextlib import ExitStack
+
+import concourse.mybir as mybir
+
+K, T, S, H, N = 1024, 4096, 2048, 512, 768
+P1, P2, P3 = 1024, 512, 256
+FLOPS = 2 * K * H * S + 2 * H * N * P3
+
+F32 = mybir.dt.float32
+BF16 = mybir.dt.bfloat16
+I32 = mybir.dt.int32
+U32 = mybir.dt.uint32
+U16 = mybir.dt.uint16
+U8 = mybir.dt.uint8
+FP8X4 = mybir.dt.float8_e4m3fn_x4
+FP4X4 = mybir.dt.float4_e2m1fn_x4
+ALU = mybir.AluOpType
+ACT = mybir.ActivationFunctionType
+
+P = 128
+PACK = 4
+PASSES = K // (P * PACK)
+BANK = 512
+SLICES = S // BANK
+LANES = 16
+
+
+def tile_list_moot_bracket_scores_kernel(
+    tc, tab_words, tab_scales, offs, pos1, pos2, pos3, pos4, pos5, pos6, w1, freq, gain, w4_words, w4_scales, out
+):
+    nc = tc.nc
+    with ExitStack() as ctx:
+        keep = ctx.enter_context(tc.tile_pool(name="keep", bufs=1))
+        ring = ctx.enter_context(tc.tile_pool(name="ring", bufs=2))
+        psum = ctx.enter_context(tc.psum_pool(name="psum", bufs=8))
+
+        def load_list(name, src):
+            tile = keep.tile(list(src.shape), U16, name=name)
+            nc.sync.dma_start(tile[:], src)
+            return tile
+
+        def entries(lst, first, count):
+            return lst[:, first // LANES : (first + count) // LANES]
+
+        offs_t = load_list("offs_t", offs)
+        tab_rows = keep.tile([P, T], U8, name="tab_rows", align_bytes=64)
+        nc.sync.dma_start(tab_rows[0:32, :].bitcast(I32), tab_scales.rearrange("a q t -> (a q) t").bitcast(I32))
+        nc.vector.memset(tab_rows[32:64, :].bitcast(I32), 0)
+        nc.vector.memset(tab_rows[64:P, :].bitcast(I32), 0)
+        freq_t = keep.tile([P, PACK], F32, name="freq_t")
+        nc.sync.dma_start(freq_t[:], freq.rearrange("(p t) -> p t", t=PACK))
+        words = [keep.tile([P, T], I32, name="words%d" % a) for a in range(PASSES)]
+        w1_raw = [keep.tile([P, PACK, H], F32, name="w1_raw%d" % a) for a in range(PASSES)]
+
+        def load_words(a):
+            nc.sync.dma_start(words[a][:], tab_words[a].rearrange("p t i -> p (t i)").bitcast(I32))
+
+        load_words(0)
+        for a in range(PASSES):
+            nc.sync.dma_start(w1_raw[a][:], w1[512 * a : 512 * (a + 1), :].rearrange("(p j) c -> p j c", j=PACK))
+        load_words(1)
+        p1_t = load_list("p1_t", pos1)
+        p2_t = load_list("p2_t", pos2)
+        p3_t = load_list("p3_t", pos3)
+        p4_t = load_list("p4_t", pos4)
+        p5_t = load_list("p5_t", pos5)
+        p6_t = load_list("p6_t", pos6)
+        gain_t = keep.tile([P, PACK], F32, name="gain_t")
+        nc.sync.dma_start(gain_t[:], gain.rearrange("(p t) -> p t", t=PACK))
+        w4_codes = keep.tile([P, 2 * N], U8, name="w4_codes", align_bytes=64)
+        nc.sync.dma_start(w4_codes[:].bitcast(I32), w4_words[0].bitcast(I32))
+        w4_plane = keep.tile([P, N], U8, name="w4_plane", align_bytes=64)
+        nc.gpsimd.memset(w4_plane[:].bitcast(I32), 0)
+        for q in range(4):
+            nc.sync.dma_start(
+                w4_plane[32 * q : 32 * q + 4, :].bitcast(I32), w4_scales[0, 4 * q : 4 * q + 4, :].bitcast(I32)
+            )
+
+        turns_t = keep.tile([P, PACK], F32, name="turns_t")
+        nc.scalar.mul(turns_t[:], freq_t[:], 1.0 / (2.0 * math.pi))
+
+        v_rows = keep.tile([P, S], U8, name="v_rows", align_bytes=64)
+        nc.vector.tensor_copy(v_rows[:], tab_rows[:].indirect(offs_t[:]))
+        v_plane = keep.tile([P, S], U8, name="v_plane", align_bytes=64)
+        nc.gpsimd.memset(v_plane[:].bitcast(I32), 0)
+        for a in range(PASSES):
+            for q in range(4):
+                nc.gpsimd.dma_start(
+                    v_plane[32 * q + 4 * a : 32 * q + 4 * a + 4, :].bitcast(I32),
+                    v_rows[16 * a + 4 * q : 16 * a + 4 * q + 4, :].bitcast(I32),
+                )
+        v_codes0 = keep.tile([P, S], U32, name="v_codes0", align_bytes=64)
+        nc.vector.tensor_copy(v_codes0[:], words[0][:].bitcast(U32).indirect(offs_t[:]))
+
+        w1_codes, w1_plane = [], []
+        for a in range(PASSES):
+            grouped = keep.tile([P, PACK, P, PACK], BF16, name="w1_grouped%d" % a, align_bytes=64)
+            nc.scalar.copy(
+                grouped[:].rearrange("p t m j -> p m j t"), w1_raw[a][:].rearrange("p j (m t) -> p m j t", t=PACK)
+            )
+            codes = keep.tile([P, H], U32, name="w1_codes%d" % a, align_bytes=64)
+            plane = keep.tile([P, H], U8, name="w1_plane%d" % a, align_bytes=64)
+            nc.vector.quantize_mx(
+                out=codes[:].bitcast(FP8X4), scales=plane[:], in_=grouped[:].rearrange("p t m j -> p (t m j)")
+            )
+            w1_codes.append(codes)
+            w1_plane.append(plane)
+
+        v_codes1 = []
+        for s in range(SLICES):
+            piece = keep.tile([P, BANK], U32, name="v_codes1_%d" % s, align_bytes=64)
+            nc.vector.tensor_copy(piece[:], words[1][:].bitcast(U32).indirect(entries(offs_t, s * BANK, BANK)))
+            v_codes1.append(piece)
+
+        folded = [keep.tile([P, S], F32, name="folded%d" % t) for t in range(PACK)]
+        whole = [keep.tile([P, S], U32, name="whole%d" % t) for t in range(PACK)]
+        h = [keep.tile([P, S], F32, name="h%d" % t) for t in range(PACK)]
+        first = {}
+        duel = {}
+        bench = [keep.tile([P, P2], F32, name="bench%d" % t) for t in range(PACK)]
+        spare = keep.tile([P, 2 * P2 + P3], F32, name="spare")
+        bracket = keep.tile([P, PACK, P3], F32, name="bracket")
+        squashed = keep.tile([P, PACK, P3], F32, name="squashed")
+
+        def product_and_fold(t, s):
+            cols = slice(s * BANK, (s + 1) * BANK)
+            rows = slice(t * P, (t + 1) * P)
+            acc = psum.tile([P, BANK], F32, name="acc")
+            for a in range(PASSES):
+                moving = v_codes0[:, cols] if a == 0 else v_codes1[s][:]
+                nc.tensor.matmul_mx(
+                    out=acc[:],
+                    lhsT=w1_codes[a][:, rows].bitcast(FP8X4),
+                    lhsT_scale=w1_plane[a][:, rows],
+                    rhs=moving.bitcast(FP8X4),
+                    rhs_scale=v_plane[4 * a : P, cols],
+                    start=(a == 0),
+                    stop=(a == PASSES - 1),
+                )
+            nc.scalar.activation(folded[t][:, cols], acc[:], ACT.Abs, bias=-0.25, scale=turns_t[:, t : t + 1])
+
+        def count_turns(t, cols):
+            nc.scalar.activation(whole[t][:, cols], folded[t][:, cols], ACT.Copy, bias=-0.25)
+
+        def reduce_turns(t, cols):
+            nc.vector.scalar_tensor_tensor(
+                h[t][:, cols], whole[t][:, cols].bitcast(I32), 0.25, folded[t][:, cols], ALU.add, ALU.subtract
+            )
+
+        def sine(t, cols):
+            nc.scalar.activation(h[t][:, cols], h[t][:, cols], ACT.Sin, scale=2.0 * math.pi)
+
+        halves = [slice(0, S // 2), slice(S // 2, S)]
+
+        def fold_tile(t):
+            for s in range(SLICES):
+                product_and_fold(t, s)
+            count_turns(t, slice(0, S))
+
+        def finish_features(t):
+            for cols in halves:
+                reduce_turns(t, cols)
+            for cols in halves:
+                sine(t, cols)
+
+        def level1(t):
+            half = P1 // 2
+            first[t] = ring.tile([P, P1], F32, name="first")
+            duel[t] = ring.tile([P, P1], F32, name="duel")
+            for u in range(2):
+                nc.vector.tensor_copy(
+                    first[t][:, u * half : (u + 1) * half], h[t][:].indirect(entries(p1_t, u * half, half))
+                )
+            for u in range(2):
+                cols = slice(u * half, (u + 1) * half)
+                nc.vector.tensor_tensor(
+                    duel[t][:, cols], h[t][:].indirect(entries(p2_t, u * half, half)), first[t][:, cols], ALU.mult
+                )
+
+        for s in range(SLICES):
+            product_and_fold(0, s)
+            count_turns(0, slice(s * BANK, (s + 1) * BANK))
+        finish_features(0)
+        fold_tile(1)
+
+        for t in range(PACK):
+            level1(t)
+            if t + 1 < PACK:
+                finish_features(t + 1)
+                scratch = folded[t + 1]
+                pick5 = scratch[:, 0:P3]
+                pick3 = scratch[:, P3 : P3 + P2]
+                pick4 = whole[t + 1][:, 0:P2].bitcast(F32)
+            else:
+                pick5 = first[t][:, 0:P3]
+                pick3 = spare[:, 0:P2]
+                pick4 = spare[:, P2 : 2 * P2]
+            if t + 2 < PACK:
+                fold_tile(t + 2)
+            if t > 0:
+                nc.vector.tensor_copy(pick5, bench[t - 1][:].indirect(p5_t[:]))
+            nc.vector.tensor_copy(pick3, duel[t][:].indirect(p3_t[:]))
+            nc.vector.tensor_copy(pick4, duel[t][:].indirect(p4_t[:]))
+            if t > 0:
+                nc.vector.tensor_tensor(bracket[:, t - 1, :], bench[t - 1][:].indirect(p6_t[:]), pick5, ALU.add)
+            nc.vector.tensor_tensor(bench[t][:], pick3, pick4, ALU.max)
+        last = PACK - 1
+        pick5 = spare[:, 2 * P2 : 2 * P2 + P3]
+        part = P3 // 2
+        parts = [slice(u * part, (u + 1) * part) for u in range(2)]
+        for u in range(2):
+            nc.vector.tensor_copy(pick5[:, parts[u]], bench[last][:].indirect(entries(p5_t, u * part, part)))
+        for u in range(2):
+            nc.vector.tensor_tensor(
+                bracket[:, last, parts[u]],
+                bench[last][:].indirect(entries(p6_t, u * part, part)),
+                pick5[:, parts[u]],
+                ALU.add,
+            )
+
+        nc.scalar.activation(squashed[:, 0:last, :], bracket[:, 0:last, :], ACT.Tanh)
+        z = [keep.tile([P, part, PACK], BF16, name="z%d" % u, align_bytes=64) for u in range(2)]
+        for t in range(last):
+            for u in range(2):
+                nc.scalar.activation(z[u][:, :, t], squashed[:, t, parts[u]], ACT.Copy, scale=gain_t[:, t : t + 1])
+
+        groups = N // P // 2
+        for u in range(2):
+            nc.scalar.activation(squashed[:, last, parts[u]], bracket[:, last, parts[u]], ACT.Tanh)
+            nc.scalar.activation(
+                z[u][:, :, last], squashed[:, last, parts[u]], ACT.Copy, scale=gain_t[:, last : last + 1]
+            )
+            z_codes = keep.tile([P, part], U32, name="z_codes%d" % u, align_bytes=64)
+            z_plane = keep.tile([P, part], U8, name="z_plane%d" % u, align_bytes=64)
+            nc.vector.quantize_mx(
+                out=z_codes[:].bitcast(FP8X4), scales=z_plane[:], in_=z[u][:].rearrange("p j t -> p (j t)")
+            )
+            for b in range(2):
+                acc = psum.tile([P, groups, part], F32, name="acc")
+                for g in range(groups):
+                    n0 = (groups * b + g) * P
+                    nc.tensor.matmul_mx(
+                        out=acc[:, g, :],
+                        lhsT=w4_codes[:, 2 * n0 : 2 * (n0 + P)].bitcast(FP4X4),
+                        lhsT_scale=w4_plane[:, n0 : n0 + P],
+                        rhs=z_codes[:].bitcast(FP8X4),
+                        rhs_scale=z_plane[:],
+                        start=True,
+                        stop=True,
+                    )
+                scores = keep.tile([P, groups, part], F32, name="scores%d_%d" % (u, b))
+                if b == 1:
+                    nc.scalar.copy(scores[:], acc[:])
+                else:
+                    nc.vector.tensor_copy(scores[:], acc[:])
+                rows = out[groups * b * P : groups * (b + 1) * P, parts[u]]
+                nc.sync.dma_start(rows.rearrange("(g p) j -> p g j", p=P), scores[:])

@@ -45,35 +45,45 @@ def tile_list_moot_bracket_scores_kernel(
 
         offs_t = load_list("offs_t", offs)
         tab_rows = keep.tile([P, T], U8, name="tab_rows", align_bytes=64)
-        nc.sync.dma_start(tab_rows[0:32, :].bitcast(I32), tab_scales.rearrange("a q t -> (a q) t").bitcast(I32))
+        for a in range(PASSES):
+            nc.sync.dma_start(
+                tab_rows[16 * a : 16 * (a + 1), :].bitcast(I32),
+                tab_scales[a].rearrange("(q r) t -> r q t", r=4).bitcast(I32),
+            )
         nc.vector.memset(tab_rows[32:64, :].bitcast(I32), 0)
         nc.vector.memset(tab_rows[64:P, :].bitcast(I32), 0)
-        freq_t = keep.tile([P, PACK], F32, name="freq_t")
-        nc.sync.dma_start(freq_t[:], freq.rearrange("(p t) -> p t", t=PACK))
         words = [keep.tile([P, T], I32, name="words%d" % a) for a in range(PASSES)]
         w1_raw = [keep.tile([P, PACK, H], F32, name="w1_raw%d" % a) for a in range(PASSES)]
 
         def load_words(a):
             nc.sync.dma_start(words[a][:], tab_words[a].rearrange("p t i -> p (t i)").bitcast(I32))
 
-        load_words(0)
-        for a in range(PASSES):
+        def load_w1(a):
             nc.sync.dma_start(w1_raw[a][:], w1[512 * a : 512 * (a + 1), :].rearrange("(p j) c -> p j c", j=PACK))
-        load_words(1)
+
+        load_words(0)
+        load_w1(0)
         p1_t = load_list("p1_t", pos1)
         p2_t = load_list("p2_t", pos2)
         p3_t = load_list("p3_t", pos3)
         p4_t = load_list("p4_t", pos4)
         p5_t = load_list("p5_t", pos5)
         p6_t = load_list("p6_t", pos6)
+        load_w1(1)
+        load_words(1)
+
+        freq_t = keep.tile([P, PACK], F32, name="freq_t")
+        nc.gpsimd.dma_start(freq_t[:], freq.rearrange("(p t) -> p t", t=PACK))
         gain_t = keep.tile([P, PACK], F32, name="gain_t")
-        nc.sync.dma_start(gain_t[:], gain.rearrange("(p t) -> p t", t=PACK))
-        w4_codes = keep.tile([P, 2 * N], U8, name="w4_codes", align_bytes=64)
-        nc.sync.dma_start(w4_codes[:].bitcast(I32), w4_words[0].bitcast(I32))
+        nc.gpsimd.dma_start(gain_t[:], gain.rearrange("(p t) -> p t", t=PACK))
+        v_plane = keep.tile([P, S], U8, name="v_plane", align_bytes=64)
+        nc.gpsimd.memset(v_plane[:].bitcast(I32), 0)
         w4_plane = keep.tile([P, N], U8, name="w4_plane", align_bytes=64)
         nc.gpsimd.memset(w4_plane[:].bitcast(I32), 0)
+        w4_codes = keep.tile([P, 2 * N], U8, name="w4_codes", align_bytes=64)
+        nc.gpsimd.dma_start(w4_codes[:].bitcast(I32), w4_words[0].bitcast(I32))
         for q in range(4):
-            nc.sync.dma_start(
+            nc.gpsimd.dma_start(
                 w4_plane[32 * q : 32 * q + 4, :].bitcast(I32), w4_scales[0, 4 * q : 4 * q + 4, :].bitcast(I32)
             )
 
@@ -82,23 +92,16 @@ def tile_list_moot_bracket_scores_kernel(
 
         v_rows = keep.tile([P, S], U8, name="v_rows", align_bytes=64)
         nc.vector.tensor_copy(v_rows[:], tab_rows[:].indirect(offs_t[:]))
-        v_plane = keep.tile([P, S], U8, name="v_plane", align_bytes=64)
-        nc.gpsimd.memset(v_plane[:].bitcast(I32), 0)
-        for a in range(PASSES):
-            for q in range(4):
-                nc.gpsimd.dma_start(
-                    v_plane[32 * q + 4 * a : 32 * q + 4 * a + 4, :].bitcast(I32),
-                    v_rows[16 * a + 4 * q : 16 * a + 4 * q + 4, :].bitcast(I32),
-                )
+        for q in range(4):
+            nc.sync.dma_start(v_plane[32 * q : 32 * q + 8, :].bitcast(I32), v_rows[q:32:4, :].bitcast(I32))
         v_codes0 = keep.tile([P, S], U32, name="v_codes0", align_bytes=64)
         nc.vector.tensor_copy(v_codes0[:], words[0][:].bitcast(U32).indirect(offs_t[:]))
 
         w1_codes, w1_plane = [], []
         for a in range(PASSES):
             grouped = keep.tile([P, PACK, P, PACK], BF16, name="w1_grouped%d" % a, align_bytes=64)
-            nc.scalar.copy(
-                grouped[:].rearrange("p t m j -> p m j t"), w1_raw[a][:].rearrange("p j (m t) -> p m j t", t=PACK)
-            )
+            cast = nc.scalar.copy if a == 0 else nc.vector.tensor_copy
+            cast(grouped[:], w1_raw[a][:].rearrange("p j (m t) -> p t m j", t=PACK))
             codes = keep.tile([P, H], U32, name="w1_codes%d" % a, align_bytes=64)
             plane = keep.tile([P, H], U8, name="w1_plane%d" % a, align_bytes=64)
             nc.vector.quantize_mx(
@@ -181,7 +184,11 @@ def tile_list_moot_bracket_scores_kernel(
         for s in range(SLICES):
             product_and_fold(0, s)
             count_turns(0, slice(s * BANK, (s + 1) * BANK))
-        finish_features(0)
+        pieces = [slice(0, 2 * BANK), slice(2 * BANK, 3 * BANK), slice(3 * BANK, S)]
+        for cols in pieces:
+            reduce_turns(0, cols)
+        for cols in pieces:
+            sine(0, cols)
         fold_tile(1)
 
         for t in range(PACK):

@@ -2,6 +2,7 @@ import math
 from contextlib import ExitStack
 
 import concourse.mybir as mybir
+from concourse.masks import make_identity
 
 K, T, S, H, N = 1024, 4096, 2048, 512, 768
 P1, P2, P3 = 1024, 512, 256
@@ -20,7 +21,12 @@ ACT = mybir.ActivationFunctionType
 
 P = 128
 PACK = 4
-PASSES = K // (P * PACK)
+K_PASS = P * PACK
+PASSES = K // K_PASS
+QUADRANT = 32
+QUADRANTS = P // QUADRANT
+SCALE_ROWS = 4
+PASS_ROWS = QUADRANTS * SCALE_ROWS
 BANK = 512
 SLICES = S // BANK
 LANES = 16
@@ -33,25 +39,31 @@ def tile_list_moot_bracket_scores_kernel(
     with ExitStack() as ctx:
         keep = ctx.enter_context(tc.tile_pool(name="keep", bufs=1))
         ring = ctx.enter_context(tc.tile_pool(name="ring", bufs=2))
-        psum = ctx.enter_context(tc.psum_pool(name="psum", bufs=8))
+        shared = ctx.enter_context(tc.tile_pool(name="shared", bufs=1))
+        psum = ctx.enter_context(tc.psum_pool(name="psum", bufs=4))
+        turn_psum = ctx.enter_context(tc.psum_pool(name="turn_psum", bufs=2))
 
         def load_list(name, src):
             tile = keep.tile(list(src.shape), U16, name=name)
             nc.sync.dma_start(tile[:], src)
             return tile
 
-        def entries(lst, first, count):
-            return lst[:, first // LANES : (first + count) // LANES]
+        def entries(lst, start, count):
+            return lst[:, start // LANES : (start + count) // LANES]
+
+        def slice_cols(s):
+            return slice(s * BANK, (s + 1) * BANK)
 
         offs_t = load_list("offs_t", offs)
-        tab_rows = keep.tile([P, T], U8, name="tab_rows", align_bytes=64)
+        staged = PASSES * PASS_ROWS
+        tab_rows = shared.tile([P, T], U8, name="tab_rows", align_bytes=64, offset=0)
         for a in range(PASSES):
             nc.sync.dma_start(
-                tab_rows[16 * a : 16 * (a + 1), :].bitcast(I32),
-                tab_scales[a].rearrange("(q r) t -> r q t", r=4).bitcast(I32),
+                tab_rows[PASS_ROWS * a : PASS_ROWS * (a + 1), :].bitcast(I32),
+                tab_scales[a].rearrange("(q e) t -> e q t", e=SCALE_ROWS).bitcast(I32),
             )
-        nc.vector.memset(tab_rows[32:64, :].bitcast(I32), 0)
-        nc.vector.memset(tab_rows[64:P, :].bitcast(I32), 0)
+        nc.vector.memset(tab_rows[staged : 2 * QUADRANT, :].bitcast(I32), 0)
+        nc.vector.memset(tab_rows[2 * QUADRANT : P, :].bitcast(I32), 0)
         words = [keep.tile([P, T], I32, name="words%d" % a) for a in range(PASSES)]
         w1_raw = [keep.tile([P, PACK, H], F32, name="w1_raw%d" % a) for a in range(PASSES)]
 
@@ -59,53 +71,66 @@ def tile_list_moot_bracket_scores_kernel(
             nc.sync.dma_start(words[a][:], tab_words[a].rearrange("p t i -> p (t i)").bitcast(I32))
 
         def load_w1(a):
-            nc.sync.dma_start(w1_raw[a][:], w1[512 * a : 512 * (a + 1), :].rearrange("(p j) c -> p j c", j=PACK))
+            k_rows = w1[K_PASS * a : K_PASS * (a + 1), :]
+            nc.sync.dma_start(w1_raw[a][:], k_rows.rearrange("(p i) c -> p i c", i=PACK))
 
         load_words(0)
         load_w1(0)
+        freq_t = keep.tile([P, PACK], F32, name="freq_t")
+        nc.sync.dma_start(freq_t[:], freq.rearrange("(p t) -> p t", t=PACK))
         p1_t = load_list("p1_t", pos1)
         p2_t = load_list("p2_t", pos2)
         p3_t = load_list("p3_t", pos3)
         p4_t = load_list("p4_t", pos4)
         p5_t = load_list("p5_t", pos5)
-        p6_t = load_list("p6_t", pos6)
         load_w1(1)
         load_words(1)
-
-        freq_t = keep.tile([P, PACK], F32, name="freq_t")
-        nc.gpsimd.dma_start(freq_t[:], freq.rearrange("(p t) -> p t", t=PACK))
+        p6_t = load_list("p6_t", pos6)
         gain_t = keep.tile([P, PACK], F32, name="gain_t")
-        nc.gpsimd.dma_start(gain_t[:], gain.rearrange("(p t) -> p t", t=PACK))
+        nc.sync.dma_start(gain_t[:], gain.rearrange("(p t) -> p t", t=PACK))
         v_plane = keep.tile([P, S], U8, name="v_plane", align_bytes=64)
-        nc.gpsimd.memset(v_plane[:].bitcast(I32), 0)
-        w4_plane = keep.tile([P, N], U8, name="w4_plane", align_bytes=64)
-        nc.gpsimd.memset(w4_plane[:].bitcast(I32), 0)
-        w4_codes = keep.tile([P, 2 * N], U8, name="w4_codes", align_bytes=64)
-        nc.gpsimd.dma_start(w4_codes[:].bitcast(I32), w4_words[0].bitcast(I32))
-        for q in range(4):
-            nc.gpsimd.dma_start(
-                w4_plane[32 * q : 32 * q + 4, :].bitcast(I32), w4_scales[0, 4 * q : 4 * q + 4, :].bitcast(I32)
-            )
+        nc.vector.memset(v_plane[:].bitcast(I32), 0)
 
+        ident = keep.tile([P, P], F32, name="ident")
+        make_identity(nc, ident[:])
+        unused = keep.tile([P, 1], F32, name="unused")
+        nc.scalar.activation(unused[:], freq_t[:, 0:1], ACT.Sin, scale=0.0)
         turns_t = keep.tile([P, PACK], F32, name="turns_t")
         nc.scalar.mul(turns_t[:], freq_t[:], 1.0 / (2.0 * math.pi))
 
         v_rows = keep.tile([P, S], U8, name="v_rows", align_bytes=64)
         nc.vector.tensor_copy(v_rows[:], tab_rows[:].indirect(offs_t[:]))
-        for q in range(4):
-            nc.sync.dma_start(v_plane[32 * q : 32 * q + 8, :].bitcast(I32), v_rows[q:32:4, :].bitcast(I32))
+        for q in range(QUADRANTS):
+            nc.sync.dma_start(
+                v_plane[QUADRANT * q : QUADRANT * q + PASSES * SCALE_ROWS, :].bitcast(I32),
+                v_rows[q:staged:QUADRANTS, :].bitcast(I32),
+            )
+        w4_codes = shared.tile([P, 2 * N], U8, name="w4_codes", align_bytes=64, offset=0)
+        nc.sync.dma_start(w4_codes[:].bitcast(I32), w4_words[0].bitcast(I32))
+        w4_plane = shared.tile([P, N], U8, name="w4_plane", align_bytes=64, offset=2 * N)
+        nc.vector.memset(w4_plane[:].bitcast(I32), 0)
+        for q in range(QUADRANTS):
+            nc.sync.dma_start(
+                w4_plane[QUADRANT * q : QUADRANT * q + SCALE_ROWS, :].bitcast(I32),
+                w4_scales[0, SCALE_ROWS * q : SCALE_ROWS * (q + 1), :].bitcast(I32),
+            )
         v_codes0 = keep.tile([P, S], U32, name="v_codes0", align_bytes=64)
         nc.vector.tensor_copy(v_codes0[:], words[0][:].bitcast(U32).indirect(offs_t[:]))
 
         w1_codes, w1_plane = [], []
         for a in range(PASSES):
             grouped = keep.tile([P, PACK, P, PACK], BF16, name="w1_grouped%d" % a, align_bytes=64)
-            cast = nc.scalar.copy if a == 0 else nc.vector.tensor_copy
-            cast(grouped[:], w1_raw[a][:].rearrange("p j (m t) -> p t m j", t=PACK))
+            if a == 0:
+                nc.scalar.copy(
+                    grouped[:].rearrange("p (u e) m i -> p u m i e", e=2),
+                    w1_raw[a][:].rearrange("p i (m u e) -> p u m i e", u=2, e=2),
+                )
+            else:
+                nc.vector.tensor_copy(grouped[:], w1_raw[a][:].rearrange("p i (m t) -> p t m i", t=PACK))
             codes = keep.tile([P, H], U32, name="w1_codes%d" % a, align_bytes=64)
             plane = keep.tile([P, H], U8, name="w1_plane%d" % a, align_bytes=64)
             nc.vector.quantize_mx(
-                out=codes[:].bitcast(FP8X4), scales=plane[:], in_=grouped[:].rearrange("p t m j -> p (t m j)")
+                out=codes[:].bitcast(FP8X4), scales=plane[:], in_=grouped[:].rearrange("p t m i -> p (t m i)")
             )
             w1_codes.append(codes)
             w1_plane.append(plane)
@@ -117,7 +142,7 @@ def tile_list_moot_bracket_scores_kernel(
             v_codes1.append(piece)
 
         folded = [keep.tile([P, S], F32, name="folded%d" % t) for t in range(PACK)]
-        whole = [keep.tile([P, S], U32, name="whole%d" % t) for t in range(PACK)]
+        count = [keep.tile([P, S], U32, name="count%d" % t) for t in range(PACK)]
         h = [keep.tile([P, S], F32, name="h%d" % t) for t in range(PACK)]
         first = {}
         duel = {}
@@ -127,7 +152,7 @@ def tile_list_moot_bracket_scores_kernel(
         squashed = keep.tile([P, PACK, P3], F32, name="squashed")
 
         def product_and_fold(t, s):
-            cols = slice(s * BANK, (s + 1) * BANK)
+            cols = slice_cols(s)
             rows = slice(t * P, (t + 1) * P)
             acc = psum.tile([P, BANK], F32, name="acc")
             for a in range(PASSES):
@@ -137,35 +162,84 @@ def tile_list_moot_bracket_scores_kernel(
                     lhsT=w1_codes[a][:, rows].bitcast(FP8X4),
                     lhsT_scale=w1_plane[a][:, rows],
                     rhs=moving.bitcast(FP8X4),
-                    rhs_scale=v_plane[4 * a : P, cols],
+                    rhs_scale=v_plane[SCALE_ROWS * a : P, cols],
                     start=(a == 0),
                     stop=(a == PASSES - 1),
                 )
             nc.scalar.activation(folded[t][:, cols], acc[:], ACT.Abs, bias=-0.25, scale=turns_t[:, t : t + 1])
 
-        def count_turns(t, cols):
-            nc.scalar.activation(whole[t][:, cols], folded[t][:, cols], ACT.Copy, bias=-0.25)
+        def count_on_scalar(t, cols):
+            nc.scalar.activation(count[t][:, cols], folded[t][:, cols], ACT.Copy, bias=-0.25)
 
-        def reduce_turns(t, cols):
+        def count_on_vector(t, cols):
+            nc.vector.tensor_scalar(count[t][:, cols].bitcast(I32), folded[t][:, cols], -0.25, None, ALU.add)
+
+        def subtract_on_vector(t, cols):
             nc.vector.scalar_tensor_tensor(
-                h[t][:, cols], whole[t][:, cols].bitcast(I32), 0.25, folded[t][:, cols], ALU.add, ALU.subtract
+                h[t][:, cols], count[t][:, cols].bitcast(I32), 0.25, folded[t][:, cols], ALU.add, ALU.subtract
             )
 
         def sine(t, cols):
             nc.scalar.activation(h[t][:, cols], h[t][:, cols], ACT.Sin, scale=2.0 * math.pi)
 
-        halves = [slice(0, S // 2), slice(S // 2, S)]
+        lower, upper = slice(0, S // 2), slice(S // 2, S)
+        blocks = BANK // P
 
-        def fold_tile(t):
-            for s in range(SLICES):
-                product_and_fold(t, s)
-            count_turns(t, slice(0, S))
+        def negate_count(t, cols):
+            nc.scalar.activation(h[t][:, cols], count[t][:, cols], ACT.Copy, bias=-0.25, scale=-1.0)
 
-        def finish_features(t):
-            for cols in halves:
-                reduce_turns(t, cols)
-            for cols in halves:
-                sine(t, cols)
+        def subtract_transposed(t, s):
+            bank = turn_psum.tile([P, BANK], F32, name="turned")
+            for b in range(blocks):
+                cols = slice(s * BANK + b * P, s * BANK + (b + 1) * P)
+                for step, src in enumerate((folded[t], h[t])):
+                    nc.tensor.matmul(
+                        bank[:, b * P : (b + 1) * P],
+                        src[:, cols],
+                        ident[:],
+                        start=(step == 0),
+                        stop=(step == 1),
+                        is_transpose=True,
+                    )
+            return bank
+
+        def sine_and_transpose_back(t, s, bank):
+            nc.scalar.activation(count[t][:, slice_cols(s)].bitcast(F32), bank[:], ACT.Sin, scale=-2.0 * math.pi)
+            back = turn_psum.tile([P, BANK], F32, name="back")
+            for b in range(blocks):
+                cols = slice(s * BANK + b * P, s * BANK + (b + 1) * P)
+                nc.tensor.transpose(back[:, b * P : (b + 1) * P], count[t][:, cols].bitcast(F32), ident[:])
+            return back
+
+        def keep_features(t, s, back):
+            nc.scalar.copy(h[t][:, slice_cols(s)], back[:])
+
+        def begin_transposed(t):
+            product_and_fold(t, 2)
+            count_on_scalar(t, lower)
+            product_and_fold(t, 3)
+            negate_count(t, lower)
+
+        def finish_transposed(t):
+            banks = [subtract_transposed(t, 0), subtract_transposed(t, 1)]
+            count_on_scalar(t, upper)
+            backs = [sine_and_transpose_back(t, 0, banks[0])]
+            negate_count(t, upper)
+            banks.append(subtract_transposed(t, 2))
+            backs.append(sine_and_transpose_back(t, 1, banks[1]))
+            banks.append(subtract_transposed(t, 3))
+            keep_features(t, 0, backs[0])
+            backs.append(sine_and_transpose_back(t, 2, banks[2]))
+            keep_features(t, 1, backs[1])
+            backs.append(sine_and_transpose_back(t, 3, banks[3]))
+            if t + 1 < PACK:
+                product_and_fold(t + 1, 0)
+            keep_features(t, 2, backs[2])
+            if t + 1 < PACK:
+                product_and_fold(t + 1, 1)
+            keep_features(t, 3, backs[3])
+            if t + 1 < PACK:
+                begin_transposed(t + 1)
 
         def level1(t):
             half = P1 // 2
@@ -183,60 +257,74 @@ def tile_list_moot_bracket_scores_kernel(
 
         for s in range(SLICES):
             product_and_fold(0, s)
-            count_turns(0, slice(s * BANK, (s + 1) * BANK))
-        pieces = [slice(0, 2 * BANK), slice(2 * BANK, 3 * BANK), slice(3 * BANK, S)]
-        for cols in pieces:
-            reduce_turns(0, cols)
+            product_and_fold(1, s)
+        pieces = [lower, slice_cols(2), slice_cols(3)]
+        count_on_vector(0, pieces[0])
+        count_on_vector(0, pieces[1])
+        subtract_on_vector(0, pieces[0])
+        count_on_vector(0, pieces[2])
+        subtract_on_vector(0, pieces[1])
+        subtract_on_vector(0, pieces[2])
         for cols in pieces:
             sine(0, cols)
-        fold_tile(1)
+        count_on_scalar(1, slice(0, S))
 
         for t in range(PACK):
             level1(t)
-            if t + 1 < PACK:
-                finish_features(t + 1)
-                scratch = folded[t + 1]
-                pick5 = scratch[:, 0:P3]
-                pick3 = scratch[:, P3 : P3 + P2]
-                pick4 = whole[t + 1][:, 0:P2].bitcast(F32)
+            if t == 0:
+                product_and_fold(2, 0)
+                product_and_fold(2, 1)
+                begin_transposed(2)
+                for cols in (lower, upper):
+                    subtract_on_vector(1, cols)
+                for cols in (lower, upper):
+                    sine(1, cols)
+                pick3 = folded[1][:, 0:P2]
+                pick4 = count[1][:, 0:P2].bitcast(F32)
             else:
+                if t + 1 < PACK:
+                    finish_transposed(t + 1)
                 pick5 = first[t][:, 0:P3]
                 pick3 = spare[:, 0:P2]
                 pick4 = spare[:, P2 : 2 * P2]
-            if t + 2 < PACK:
-                fold_tile(t + 2)
-            if t > 0:
                 nc.vector.tensor_copy(pick5, bench[t - 1][:].indirect(p5_t[:]))
             nc.vector.tensor_copy(pick3, duel[t][:].indirect(p3_t[:]))
             nc.vector.tensor_copy(pick4, duel[t][:].indirect(p4_t[:]))
             if t > 0:
                 nc.vector.tensor_tensor(bracket[:, t - 1, :], bench[t - 1][:].indirect(p6_t[:]), pick5, ALU.add)
             nc.vector.tensor_tensor(bench[t][:], pick3, pick4, ALU.max)
+
         last = PACK - 1
-        pick5 = spare[:, 2 * P2 : 2 * P2 + P3]
+        last_pick5 = spare[:, 2 * P2 : 2 * P2 + P3]
         part = P3 // 2
         parts = [slice(u * part, (u + 1) * part) for u in range(2)]
         for u in range(2):
-            nc.vector.tensor_copy(pick5[:, parts[u]], bench[last][:].indirect(entries(p5_t, u * part, part)))
+            nc.vector.tensor_copy(last_pick5[:, parts[u]], bench[last][:].indirect(entries(p5_t, u * part, part)))
         for u in range(2):
             nc.vector.tensor_tensor(
                 bracket[:, last, parts[u]],
                 bench[last][:].indirect(entries(p6_t, u * part, part)),
-                pick5[:, parts[u]],
+                last_pick5[:, parts[u]],
                 ALU.add,
             )
 
+        rounded = keep.tile([P, PACK, P3], BF16, name="rounded")
         nc.scalar.activation(squashed[:, 0:last, :], bracket[:, 0:last, :], ACT.Tanh)
-        z = [keep.tile([P, part, PACK], BF16, name="z%d" % u, align_bytes=64) for u in range(2)]
         for t in range(last):
-            for u in range(2):
-                nc.scalar.activation(z[u][:, :, t], squashed[:, t, parts[u]], ACT.Copy, scale=gain_t[:, t : t + 1])
+            nc.scalar.activation(rounded[:, t, :], squashed[:, t, :], ACT.Copy, scale=gain_t[:, t : t + 1])
+        z = [keep.tile([P, part, PACK], BF16, name="z%d" % u, align_bytes=64) for u in range(2)]
+        for u in range(2):
+            nc.scalar.activation(squashed[:, last, parts[u]], bracket[:, last, parts[u]], ACT.Tanh)
+        for u in range(2):
+            nc.scalar.activation(
+                rounded[:, last, parts[u]], squashed[:, last, parts[u]], ACT.Copy, scale=gain_t[:, last : last + 1]
+            )
 
         groups = N // P // 2
         for u in range(2):
-            nc.scalar.activation(squashed[:, last, parts[u]], bracket[:, last, parts[u]], ACT.Tanh)
-            nc.scalar.activation(
-                z[u][:, :, last], squashed[:, last, parts[u]], ACT.Copy, scale=gain_t[:, last : last + 1]
+            nc.vector.tensor_copy(
+                z[u][:].rearrange("p (c i) t -> p c t i", i=PACK),
+                rounded[:, :, parts[u]].rearrange("p t (c i) -> p c t i", i=PACK),
             )
             z_codes = keep.tile([P, part], U32, name="z_codes%d" % u, align_bytes=64)
             z_plane = keep.tile([P, part], U8, name="z_plane%d" % u, align_bytes=64)
@@ -261,5 +349,5 @@ def tile_list_moot_bracket_scores_kernel(
                     nc.scalar.copy(scores[:], acc[:])
                 else:
                     nc.vector.tensor_copy(scores[:], acc[:])
-                rows = out[groups * b * P : groups * (b + 1) * P, parts[u]]
-                nc.sync.dma_start(rows.rearrange("(g p) j -> p g j", p=P), scores[:])
+                out_rows = out[groups * b * P : groups * (b + 1) * P, parts[u]]
+                nc.sync.dma_start(out_rows.rearrange("(g p) j -> p g j", p=P), scores[:])

import math
from contextlib import ExitStack

import concourse.mybir as mybir
from concourse.masks import make_identity

K, T, S, H, N = 1024, 4096, 2048, 512, 768
P1, P2, P3 = 1024, 512, 256
FLOPS = 2 * K * H * S + 2 * H * N * P3

F32 = mybir.dt.float32
BF16 = mybir.dt.bfloat16
I32 = mybir.dt.int32
U32 = mybir.dt.uint32
U16 = mybir.dt.uint16
U8 = mybir.dt.uint8
FP8X4 = mybir.dt.float8_e4m3fn_x4
FP4X4 = mybir.dt.float4_e2m1fn_x4
ALU = mybir.AluOpType
ACT = mybir.ActivationFunctionType

P = 128
PACK = 4
K_PASS = P * PACK
PASSES = K // K_PASS
QUADRANT = 32
QUADRANTS = P // QUADRANT
SCALE_ROWS = 4
PASS_ROWS = QUADRANTS * SCALE_ROWS
BANK = 512
SLICES = S // BANK
LANES = 16


def tile_list_moot_bracket_scores_kernel(
    tc, tab_words, tab_scales, offs, pos1, pos2, pos3, pos4, pos5, pos6, w1, freq, gain, w4_words, w4_scales, out
):
    nc = tc.nc
    with ExitStack() as ctx:
        keep = ctx.enter_context(tc.tile_pool(name="keep", bufs=1))
        ring = ctx.enter_context(tc.tile_pool(name="ring", bufs=2))
        shared = ctx.enter_context(tc.tile_pool(name="shared", bufs=1))
        psum = ctx.enter_context(tc.psum_pool(name="psum", bufs=4))
        turn_psum = ctx.enter_context(tc.psum_pool(name="turn_psum", bufs=2))

        def load_list(name, src):
            tile = keep.tile(list(src.shape), U16, name=name)
            nc.sync.dma_start(tile[:], src)
            return tile

        def entries(lst, start, count):
            return lst[:, start // LANES : (start + count) // LANES]

        def slice_cols(s):
            return slice(s * BANK, (s + 1) * BANK)

        offs_t = load_list("offs_t", offs)
        staged = PASSES * PASS_ROWS
        tab_rows = shared.tile([P, T], U8, name="tab_rows", align_bytes=64, offset=0)
        for a in range(PASSES):
            nc.sync.dma_start(
                tab_rows[PASS_ROWS * a : PASS_ROWS * (a + 1), :].bitcast(I32),
                tab_scales[a].rearrange("(q e) t -> e q t", e=SCALE_ROWS).bitcast(I32),
            )
        nc.vector.memset(tab_rows[staged : 2 * QUADRANT, :].bitcast(I32), 0)
        nc.vector.memset(tab_rows[2 * QUADRANT : P, :].bitcast(I32), 0)
        words = [keep.tile([P, T], I32, name="words%d" % a) for a in range(PASSES)]
        w1_raw = [keep.tile([P, PACK, H], F32, name="w1_raw%d" % a) for a in range(PASSES)]

        def load_words(a):
            nc.sync.dma_start(words[a][:], tab_words[a].rearrange("p t i -> p (t i)").bitcast(I32))

        def load_w1(a):
            k_rows = w1[K_PASS * a : K_PASS * (a + 1), :]
            nc.sync.dma_start(w1_raw[a][:], k_rows.rearrange("(p i) c -> p i c", i=PACK))

        load_words(0)
        load_w1(0)
        freq_t = keep.tile([P, PACK], F32, name="freq_t")
        nc.sync.dma_start(freq_t[:], freq.rearrange("(p t) -> p t", t=PACK))
        p1_t = load_list("p1_t", pos1)
        p2_t = load_list("p2_t", pos2)
        p3_t = load_list("p3_t", pos3)
        p4_t = load_list("p4_t", pos4)
        p5_t = load_list("p5_t", pos5)
        load_w1(1)
        load_words(1)
        p6_t = load_list("p6_t", pos6)
        gain_t = keep.tile([P, PACK], F32, name="gain_t")
        nc.sync.dma_start(gain_t[:], gain.rearrange("(p t) -> p t", t=PACK))
        v_plane = keep.tile([P, S], U8, name="v_plane", align_bytes=64)
        nc.vector.memset(v_plane[:].bitcast(I32), 0)

        ident = keep.tile([P, P], F32, name="ident")
        make_identity(nc, ident[:])
        unused = keep.tile([P, 1], F32, name="unused")
        nc.scalar.activation(unused[:], freq_t[:, 0:1], ACT.Sin, scale=0.0)
        turns_t = keep.tile([P, PACK], F32, name="turns_t")
        nc.scalar.mul(turns_t[:], freq_t[:], 1.0 / (2.0 * math.pi))

        v_rows = keep.tile([P, S], U8, name="v_rows", align_bytes=64)
        nc.vector.tensor_copy(v_rows[:], tab_rows[:].indirect(offs_t[:]))
        for q in range(QUADRANTS):
            nc.sync.dma_start(
                v_plane[QUADRANT * q : QUADRANT * q + PASSES * SCALE_ROWS, :].bitcast(I32),
                v_rows[q:staged:QUADRANTS, :].bitcast(I32),
            )
        w4_codes = shared.tile([P, 2 * N], U8, name="w4_codes", align_bytes=64, offset=0)
        nc.sync.dma_start(w4_codes[:].bitcast(I32), w4_words[0].bitcast(I32))
        w4_plane = shared.tile([P, N], U8, name="w4_plane", align_bytes=64, offset=2 * N)
        nc.vector.memset(w4_plane[:].bitcast(I32), 0)
        for q in range(QUADRANTS):
            nc.sync.dma_start(
                w4_plane[QUADRANT * q : QUADRANT * q + SCALE_ROWS, :].bitcast(I32),
                w4_scales[0, SCALE_ROWS * q : SCALE_ROWS * (q + 1), :].bitcast(I32),
            )
        v_codes0 = keep.tile([P, S], U32, name="v_codes0", align_bytes=64)
        nc.vector.tensor_copy(v_codes0[:], words[0][:].bitcast(U32).indirect(offs_t[:]))

        w1_codes, w1_plane = [], []
        for a in range(PASSES):
            grouped = keep.tile([P, PACK, P, PACK], BF16, name="w1_grouped%d" % a, align_bytes=64)
            if a == 0:
                nc.scalar.copy(
                    grouped[:].rearrange("p (u e) m i -> p u m i e", e=2),
                    w1_raw[a][:].rearrange("p i (m u e) -> p u m i e", u=2, e=2),
                )
            else:
                nc.vector.tensor_copy(grouped[:], w1_raw[a][:].rearrange("p i (m t) -> p t m i", t=PACK))
            codes = keep.tile([P, H], U32, name="w1_codes%d" % a, align_bytes=64)
            plane = keep.tile([P, H], U8, name="w1_plane%d" % a, align_bytes=64)
            nc.vector.quantize_mx(
                out=codes[:].bitcast(FP8X4), scales=plane[:], in_=grouped[:].rearrange("p t m i -> p (t m i)")
            )
            w1_codes.append(codes)
            w1_plane.append(plane)

        v_codes1 = []
        for s in range(SLICES):
            piece = keep.tile([P, BANK], U32, name="v_codes1_%d" % s, align_bytes=64)
            nc.vector.tensor_copy(piece[:], words[1][:].bitcast(U32).indirect(entries(offs_t, s * BANK, BANK)))
            v_codes1.append(piece)

        folded = [keep.tile([P, S], F32, name="folded%d" % t) for t in range(PACK)]
        count = [keep.tile([P, S], U32, name="count%d" % t) for t in range(PACK)]
        h = [keep.tile([P, S], F32, name="h%d" % t) for t in range(PACK)]
        first = {}
        duel = {}
        bench = [keep.tile([P, P2], F32, name="bench%d" % t) for t in range(PACK)]
        spare = keep.tile([P, 2 * P2 + P3], F32, name="spare")
        bracket = keep.tile([P, PACK, P3], F32, name="bracket")
        squashed = keep.tile([P, PACK, P3], F32, name="squashed")

        def product_and_fold(t, s):
            cols = slice_cols(s)
            rows = slice(t * P, (t + 1) * P)
            acc = psum.tile([P, BANK], F32, name="acc")
            for a in range(PASSES):
                moving = v_codes0[:, cols] if a == 0 else v_codes1[s][:]
                nc.tensor.matmul_mx(
                    out=acc[:],
                    lhsT=w1_codes[a][:, rows].bitcast(FP8X4),
                    lhsT_scale=w1_plane[a][:, rows],
                    rhs=moving.bitcast(FP8X4),
                    rhs_scale=v_plane[SCALE_ROWS * a : P, cols],
                    start=(a == 0),
                    stop=(a == PASSES - 1),
                )
            nc.scalar.activation(folded[t][:, cols], acc[:], ACT.Abs, bias=-0.25, scale=turns_t[:, t : t + 1])

        def count_on_scalar(t, cols):
            nc.scalar.activation(count[t][:, cols], folded[t][:, cols], ACT.Copy, bias=-0.25)

        def count_on_vector(t, cols):
            nc.vector.tensor_scalar(count[t][:, cols].bitcast(I32), folded[t][:, cols], -0.25, None, ALU.add)

        def subtract_on_vector(t, cols):
            nc.vector.scalar_tensor_tensor(
                h[t][:, cols], count[t][:, cols].bitcast(I32), 0.25, folded[t][:, cols], ALU.add, ALU.subtract
            )

        def sine(t, cols):
            nc.scalar.activation(h[t][:, cols], h[t][:, cols], ACT.Sin, scale=2.0 * math.pi)

        lower, upper = slice(0, S // 2), slice(S // 2, S)
        blocks = BANK // P

        def negate_count(t, cols):
            nc.scalar.activation(h[t][:, cols], count[t][:, cols], ACT.Copy, bias=-0.25, scale=-1.0)

        def subtract_transposed(t, s):
            bank = turn_psum.tile([P, BANK], F32, name="turned")
            for b in range(blocks):
                cols = slice(s * BANK + b * P, s * BANK + (b + 1) * P)
                for step, src in enumerate((folded[t], h[t])):
                    nc.tensor.matmul(
                        bank[:, b * P : (b + 1) * P],
                        src[:, cols],
                        ident[:],
                        start=(step == 0),
                        stop=(step == 1),
                        is_transpose=True,
                    )
            return bank

        def sine_and_transpose_back(t, s, bank):
            nc.scalar.activation(count[t][:, slice_cols(s)].bitcast(F32), bank[:], ACT.Sin, scale=-2.0 * math.pi)
            back = turn_psum.tile([P, BANK], F32, name="back")
            for b in range(blocks):
                cols = slice(s * BANK + b * P, s * BANK + (b + 1) * P)
                nc.tensor.transpose(back[:, b * P : (b + 1) * P], count[t][:, cols].bitcast(F32), ident[:])
            return back

        def keep_features(t, s, back):
            nc.scalar.copy(h[t][:, slice_cols(s)], back[:])

        def begin_transposed(t):
            product_and_fold(t, 2)
            count_on_scalar(t, lower)
            product_and_fold(t, 3)
            negate_count(t, lower)

        def finish_transposed(t):
            banks = [subtract_transposed(t, 0), subtract_transposed(t, 1)]
            count_on_scalar(t, upper)
            backs = [sine_and_transpose_back(t, 0, banks[0])]
            negate_count(t, upper)
            banks.append(subtract_transposed(t, 2))
            backs.append(sine_and_transpose_back(t, 1, banks[1]))
            banks.append(subtract_transposed(t, 3))
            keep_features(t, 0, backs[0])
            backs.append(sine_and_transpose_back(t, 2, banks[2]))
            keep_features(t, 1, backs[1])
            backs.append(sine_and_transpose_back(t, 3, banks[3]))
            if t + 1 < PACK:
                product_and_fold(t + 1, 0)
            keep_features(t, 2, backs[2])
            if t + 1 < PACK:
                product_and_fold(t + 1, 1)
            keep_features(t, 3, backs[3])
            if t + 1 < PACK:
                begin_transposed(t + 1)

        def level1(t):
            half = P1 // 2
            first[t] = ring.tile([P, P1], F32, name="first")
            duel[t] = ring.tile([P, P1], F32, name="duel")
            for u in range(2):
                nc.vector.tensor_copy(
                    first[t][:, u * half : (u + 1) * half], h[t][:].indirect(entries(p1_t, u * half, half))
                )
            for u in range(2):
                cols = slice(u * half, (u + 1) * half)
                nc.vector.tensor_tensor(
                    duel[t][:, cols], h[t][:].indirect(entries(p2_t, u * half, half)), first[t][:, cols], ALU.mult
                )

        for s in range(SLICES):
            product_and_fold(0, s)
            product_and_fold(1, s)
        pieces = [lower, slice_cols(2), slice_cols(3)]
        count_on_vector(0, pieces[0])
        count_on_vector(0, pieces[1])
        subtract_on_vector(0, pieces[0])
        count_on_vector(0, pieces[2])
        subtract_on_vector(0, pieces[1])
        subtract_on_vector(0, pieces[2])
        for cols in pieces:
            sine(0, cols)
        count_on_scalar(1, slice(0, S))

        for t in range(PACK):
            level1(t)
            if t == 0:
                product_and_fold(2, 0)
                product_and_fold(2, 1)
                begin_transposed(2)
                for cols in (lower, upper):
                    subtract_on_vector(1, cols)
                for cols in (lower, upper):
                    sine(1, cols)
                pick3 = folded[1][:, 0:P2]
                pick4 = count[1][:, 0:P2].bitcast(F32)
            else:
                if t + 1 < PACK:
                    finish_transposed(t + 1)
                pick5 = first[t][:, 0:P3]
                pick3 = spare[:, 0:P2]
                pick4 = spare[:, P2 : 2 * P2]
                nc.vector.tensor_copy(pick5, bench[t - 1][:].indirect(p5_t[:]))
            nc.vector.tensor_copy(pick3, duel[t][:].indirect(p3_t[:]))
            nc.vector.tensor_copy(pick4, duel[t][:].indirect(p4_t[:]))
            if t > 0:
                nc.vector.tensor_tensor(bracket[:, t - 1, :], bench[t - 1][:].indirect(p6_t[:]), pick5, ALU.add)
            nc.vector.tensor_tensor(bench[t][:], pick3, pick4, ALU.max)

        last = PACK - 1
        last_pick5 = spare[:, 2 * P2 : 2 * P2 + P3]
        part = P3 // 2
        parts = [slice(u * part, (u + 1) * part) for u in range(2)]
        for u in range(2):
            nc.vector.tensor_copy(last_pick5[:, parts[u]], bench[last][:].indirect(entries(p5_t, u * part, part)))
        for u in range(2):
            nc.vector.tensor_tensor(
                bracket[:, last, parts[u]],
                bench[last][:].indirect(entries(p6_t, u * part, part)),
                last_pick5[:, parts[u]],
                ALU.add,
            )

        rounded = keep.tile([P, PACK, P3], BF16, name="rounded")
        nc.scalar.activation(squashed[:, 0:last, :], bracket[:, 0:last, :], ACT.Tanh)
        for t in range(last):
            nc.scalar.activation(rounded[:, t, :], squashed[:, t, :], ACT.Copy, scale=gain_t[:, t : t + 1])
        z = [keep.tile([P, part, PACK], BF16, name="z%d" % u, align_bytes=64) for u in range(2)]
        for u in range(2):
            nc.scalar.activation(squashed[:, last, parts[u]], bracket[:, last, parts[u]], ACT.Tanh)
        for u in range(2):
            nc.scalar.activation(
                rounded[:, last, parts[u]], squashed[:, last, parts[u]], ACT.Copy, scale=gain_t[:, last : last + 1]
            )

        groups = N // P // 2
        for u in range(2):
            nc.vector.tensor_copy(
                z[u][:].rearrange("p (c i) t -> p c t i", i=PACK),
                rounded[:, :, parts[u]].rearrange("p t (c i) -> p c t i", i=PACK),
            )
            z_codes = keep.tile([P, part], U32, name="z_codes%d" % u, align_bytes=64)
            z_plane = keep.tile([P, part], U8, name="z_plane%d" % u, align_bytes=64)
            nc.vector.quantize_mx(
                out=z_codes[:].bitcast(FP8X4), scales=z_plane[:], in_=z[u][:].rearrange("p j t -> p (j t)")
            )
            for b in range(2):
                acc = psum.tile([P, groups, part], F32, name="acc")
                for g in range(groups):
                    n0 = (groups * b + g) * P
                    nc.tensor.matmul_mx(
                        out=acc[:, g, :],
                        lhsT=w4_codes[:, 2 * n0 : 2 * (n0 + P)].bitcast(FP4X4),
                        lhsT_scale=w4_plane[:, n0 : n0 + P],
                        rhs=z_codes[:].bitcast(FP8X4),
                        rhs_scale=z_plane[:],
                        start=True,
                        stop=True,
                    )
                scores = keep.tile([P, groups, part], F32, name="scores%d_%d" % (u, b))
                if b == 1:
                    nc.scalar.copy(scores[:], acc[:])
                else:
                    nc.vector.tensor_copy(scores[:], acc[:])
                out_rows = out[groups * b * P : groups * (b + 1) * P, parts[u]]
                nc.sync.dma_start(out_rows.rearrange("(g p) j -> p g j", p=P), scores[:])
